import numpy as np
import ml_dtypes


def mxq(x, axis, fmt="e4m3"):
    dtype, down = {"e4m3": (ml_dtypes.float8_e4m3fn, 7), "e5m2": (ml_dtypes.float8_e5m2, 14)}[fmt]
    v = np.moveaxis(np.asarray(x, np.float32).astype(ml_dtypes.bfloat16).astype(np.float64), axis, -1)
    blocks = v.reshape(v.shape[:-1] + (-1, 32))
    amax = np.abs(blocks).max(-1, keepdims=True)
    byte = np.maximum(np.where(amax > 0, np.frexp(amax)[1] - 1 + 127, 0) - down, 1)
    scale = np.exp2(byte - 127.0)
    codes = (blocks / scale).astype(np.float32).astype(dtype).astype(np.float64)
    return np.moveaxis((codes * scale).reshape(v.shape), -1, axis)


WIDE = False


def mx_kscale(k, group=512):
    if not WIDE:
        return np.ones(k)
    levels = np.array([10, -10, 5, -5, 0])
    if group != 512:
        return np.exp2(np.random.permutation(np.resize(levels, k // group))).repeat(group)
    if k % 512:
        return np.exp2(np.random.permutation(np.resize(levels, k // 32))).repeat(32)
    a = np.empty((k // 512, 16))
    for p in range(k // 512):
        a[p, :8] = np.random.permutation(np.resize(levels, 8))
        for g in range(8):
            far = levels[np.abs(levels - a[p, g]) >= 10]
            a[p, g + 8] = far[np.random.randint(len(far))]
    return np.exp2(a.ravel()).repeat(32)


def f64(x):
    return np.asarray(x).astype(np.float64)


def striped(idx):
    return np.tile(np.asarray(idx).reshape(-1, 16).T, (8, 1)).astype(np.uint16)


def unstriped(offs):
    return offs[:16].T.reshape(-1).astype(np.int64)


H, KV, D, NQ, N = 4, 4, 128, 512, 1024


def setup_inputs():
    n = np.random.standard_normal
    s = mx_kscale(D, 0)[:, None]
    u = mx_kscale(N)
    t = np.random.uniform(0.5, 2.0, N) * u
    v = n((KV, N, 128))
    return {
        "qT": (n((H, D, NQ)) * s * (0.70 / np.sqrt(D))).astype(np.float32),
        "kT": (n((KV, D, N)) / s).astype(np.float32),
        "t": t.reshape(N, 1).astype(np.float32),
        "v": (v / t[:, None]).astype(np.float32),
        "kb": (0.5 * n((N, 1))).astype(np.float32),
        "mask": (np.arange(N)[:, None] <= np.sort(np.random.randint(N // 4, N, NQ))[None, :]).astype(np.float32),
        "gn": np.tile(np.random.uniform(0.5, 2.0, 128), (128, 1)).astype(np.float32),
    }


def reference(qT, kT, t, v, kb, mask, gn):
    a = mxq(f64(kT), 1, "e4m3").transpose(0, 2, 1) @ mxq(f64(qT), 1, "e4m3")
    a = a + f64(kb)
    p = np.tanh(a)
    p = p * f64(mask)
    w = p * f64(t)
    y = mxq(w, 1, "e4m3").transpose(0, 2, 1) @ mxq(f64(v), 1, "e4m3")
    y = y / 16.0
    y = y / np.sqrt(np.mean(np.square(y), -1, keepdims=True) + 1e-5) * f64(gn)[:1]
    return y

@@ -1,0 +1,300 @@
+from contextlib import ExitStack
+
+import concourse.mybir as mybir
+
+H, D, NQ, N = 4, 128, 512, 1024
+FLOPS = 2 * 2 * H * N * NQ * D
+
+F32 = mybir.dt.float32
+BF16 = mybir.dt.bfloat16
+U32 = mybir.dt.uint32
+U8 = mybir.dt.uint8
+FP8X4 = mybir.dt.float8_e4m3fn_x4
+ACT = mybir.ActivationFunctionType
+MULT = mybir.AluOpType.mult
+
+P = 128
+PACK = 4
+ROWS = 32
+PASS = P * PACK
+BLK = 128
+BANK = 512
+SKEW = 3
+
+PHASES = [(0, 0, 128), (0, 128, 128), (0, 256, 256), (1, 0, 256), (1, 256, 256)]
+
+
+def tile_rows_a_tanh_kb_mask_onorm_kernel(tc, qT, kT, t, v, kb, mask, gn, out):
+    nc = tc.nc
+    with ExitStack() as ctx:
+        keep = ctx.enter_context(tc.tile_pool(name="keep", bufs=1))
+        psum = ctx.enter_context(tc.psum_pool(name="psum", bufs=1))
+        ctx.enter_context(tc.manual_schedule())
+
+        def sbuf(name, shape, dtype):
+            return keep.tile(shape, dtype, name=name, align_bytes=64)
+
+        def quantize(name, staged, words):
+            codes = sbuf(name + "_codes", [P, words], U32)
+            scales = sbuf(name + "_scales", [P, words], U8)
+            nc.vector.quantize_mx(out=codes[:].bitcast(FP8X4), scales=scales[:], in_=staged)
+            return codes, scales
+
+        q_rows = qT.rearrange("h (p j) q -> (h p) j q", j=PACK)
+        k_rows = kT.rearrange("h (p j) n -> (h p) j n", j=PACK)
+
+        kb_sb = sbuf("kb_sb", [P, 2, PACK], F32)
+        t_sb = sbuf("t_sb", [P, 2, PACK], F32)
+        nc.scalar.dma_start(out=kb_sb[:], in_=kb.rearrange("(c p j) o -> p c (j o)", c=2, j=PACK))
+        nc.scalar.dma_start(out=t_sb[:], in_=t.rearrange("(c p j) o -> p c (j o)", c=2, j=PACK))
+
+        q_raw, k_raw, v_raw, m_sb = {}, {}, {}, {}
+
+        def load_q(q0, width):
+            q_raw[q0] = sbuf("q_raw%d" % q0, [P, PACK, width], F32)
+            nc.sync.dma_start(out=q_raw[q0][:], in_=q_rows[:, :, q0 : q0 + width])
+
+        def load_k(c):
+            k_raw[c] = sbuf("k_raw%d" % c, [P, PACK, PASS], F32)
+            nc.sync.dma_start(out=k_raw[c][:], in_=k_rows[:, :, c * PASS : (c + 1) * PASS])
+
+        def load_mask(c, q0, width):
+            m_sb[c, q0] = sbuf("mask%d_%d" % (c, q0), [P, PACK, width], F32)
+            rows = mask[c * PASS : (c + 1) * PASS, q0 : q0 + width]
+            nc.sync.dma_start(out=m_sb[c, q0][:], in_=rows.rearrange("(p j) q -> p j q", j=PACK))
+
+        def load_v(h):
+            v_raw[h] = sbuf("v_raw%d" % h, [P, 2, PACK * D], F32)
+            nc.sync.dma_start(out=v_raw[h][:], in_=v[h].rearrange("(c p j) e -> p c (j e)", c=2, j=PACK))
+
+        load_q(0, 128)
+        load_k(0)
+        load_mask(0, 0, 128)
+        load_q(128, 128)
+        load_mask(0, 128, 128)
+        load_q(256, 256)
+        load_mask(0, 256, 256)
+        load_k(1)
+        load_v(0)
+        load_v(1)
+        load_mask(1, 0, NQ)
+        load_v(2)
+        load_v(3)
+        gn_sb = sbuf("gn_sb", [P, D], F32)
+        nc.sync.dma_start(out=gn_sb[:], in_=gn[:, :])
+
+        q_bf, q_mx, k_bf, k_mx, v_bf, v_mx = {}, {}, {}, {}, {}, {}
+
+        def round_q(q0):
+            width = q_raw[q0].shape[2]
+            q_bf[q0] = sbuf("q_bf%d" % q0, [P, width * PACK], BF16)
+            nc.vector.tensor_copy(
+                out=q_bf[q0][:].rearrange("p (g i j) -> p g j i", i=2, j=PACK),
+                in_=q_raw[q0][:].rearrange("p j (g i) -> p g j i", i=2),
+            )
+
+        def quantize_q(q0):
+            width = q_raw[q0].shape[2]
+            codes, scales = quantize("q%d" % q0, q_bf[q0][:], width)
+            for b in range(width // BLK):
+                cols = slice(b * BLK, (b + 1) * BLK)
+                q_mx[q0 // BLK + b] = (codes, scales, cols)
+
+        def round_k(c, half, copy):
+            k_bf[c, half] = sbuf("k_bf%d_%d" % (c, half), [P, 2 * P * PACK], BF16)
+            src = k_raw[c][:].rearrange("p j (s r) -> p s j r", r=PACK)
+            copy(
+                out=k_bf[c, half][:].rearrange("p (r s j) -> p s j r", r=2, j=PACK),
+                in_=src[:, :, :, 2 * half : 2 * half + 2],
+            )
+
+        def quantize_k(c, half):
+            codes, scales = quantize("k%d_%d" % (c, half), k_bf[c, half][:], 2 * P)
+            for x in range(2):
+                k_mx[c, 2 * half + x] = (codes, scales, slice(x * P, (x + 1) * P))
+
+        def round_v(h):
+            v_bf[h] = sbuf("v_bf%d" % h, [P, 2 * D * PACK], BF16)
+            nc.scalar.copy(
+                out=v_bf[h][:].rearrange("p (c g i j) -> p c g j i", c=2, i=2, j=PACK),
+                in_=v_raw[h][:].rearrange("p c (j g i) -> p c g j i", j=PACK, i=2),
+            )
+
+        def quantize_v(h):
+            v_mx[h] = quantize("v%d" % h, v_bf[h][:], 2 * D)
+
+        def scale_mask(c, key, lo, hi):
+            for r in range(PACK):
+                rows = m_sb[c, key][:, r, lo:hi]
+                nc.vector.tensor_scalar(out=rows, in0=rows, scalar1=t_sb[:, c, r : r + 1], scalar2=None, op0=MULT)
+
+        score_bank = [psum.tile([P, BANK], F32, name="score%d" % h) for h in range(H)]
+        y_bank = [psum.tile([P, BANK], F32, name="y%d" % b) for b in range(4)]
+
+        units = [(c, q0, width, h) for c, q0, width in PHASES for h in range(H)]
+        fills = []
+        base = 0
+        for u, (c, q0, width, h) in enumerate(units):
+            n = width // BLK
+            for f in range(n):
+                fills.append((base + SKEW * f, u, f))
+            base = base + n
+        fills = sorted(fills)
+        p_sb = [sbuf("p%d" % u, [P, PACK, unit[2]], F32) for u, unit in enumerate(units)]
+
+        def fill(u, f):
+            c, q0, width, h = units[u]
+            rows = slice(ROWS * h, ROWS * (h + 1))
+            slots = BANK // width
+            for x in range(slots):
+                kc, ks, kcols = k_mx[c, f * slots + x]
+                for b in range(width // BLK):
+                    qc, qs, qcols = q_mx[q0 // BLK + b]
+                    lo = x * width + b * BLK
+                    nc.tensor.matmul_mx(
+                        out=score_bank[h][:, lo : lo + BLK],
+                        lhsT=kc[rows, kcols].bitcast(FP8X4),
+                        lhsT_scale=ks[rows, kcols],
+                        rhs=qc[rows, qcols].bitcast(FP8X4),
+                        rhs_scale=qs[rows, qcols],
+                        start=True,
+                        stop=True,
+                    )
+            for x in range(slots):
+                r = f * slots + x
+                nc.scalar.activation(
+                    out=p_sb[u][:, r, :],
+                    in_=score_bank[h][:, x * width : (x + 1) * width],
+                    func=ACT.Tanh,
+                    bias=kb_sb[:, c, r : r + 1],
+                )
+
+        w_bf, w_mx = {}, {}
+
+        def weigh(u):
+            c, q0, width, h = units[u]
+            key = q0 if c == 0 else 0
+            mt = m_sb[c, key][:, :, q0 - key : q0 - key + width]
+            w_bf[u] = keep.tile([P, width * PACK], BF16, name="w_bf", tag="w_bf", bufs=4, align_bytes=64)
+            nc.vector.tensor_tensor(
+                out=w_bf[u][:].rearrange("p (g i r) -> p g r i", i=2, r=PACK),
+                in0=p_sb[u][:].rearrange("p r (g i) -> p g r i", i=2),
+                in1=mt.rearrange("p r (g i) -> p g r i", i=2),
+                op=MULT,
+            )
+
+        def quantize_w(u):
+            c, q0, width, h = units[u]
+            codes, scales = quantize("w%d" % u, w_bf[u][:], width)
+            for b in range(width // BLK):
+                w_mx[c, h, q0 // BLK + b] = (codes, scales, slice(b * BLK, (b + 1) * BLK))
+
+        first = 3 * H
+        o_sb = [sbuf("o%d" % i, [P, 2, D], F32) for i in range(2 * H)]
+        ssq = sbuf("ssq", [P, 4 * H], F32)
+        rstd = sbuf("rstd", [P, 4 * H], F32)
+
+        def y_cols(i, x):
+            lo = (i % 2) * 2 * D + x * D
+            return y_bank[i // 2][:, lo : lo + D]
+
+        def second_product(i):
+            c, q0, width, h = units[first + i]
+            vc, vs = v_mx[h]
+            for x in range(2):
+                for cc in range(2):
+                    wc, ws, wcols = w_mx[cc, h, q0 // BLK + x]
+                    vcols = slice(cc * D, (cc + 1) * D)
+                    nc.tensor.matmul_mx(
+                        out=y_cols(i, x),
+                        lhsT=wc[:, wcols].bitcast(FP8X4),
+                        lhsT_scale=ws[:, wcols],
+                        rhs=vc[:, vcols].bitcast(FP8X4),
+                        rhs_scale=vs[:, vcols],
+                        start=(cc == 0),
+                        stop=(cc == 1),
+                    )
+
+        def squares(i):
+            for x in range(2):
+                nc.scalar.activation(
+                    out=o_sb[i][:, x, :], in_=y_cols(i, x), func=ACT.Square, accum_out=ssq[:, 2 * i + x : 2 * i + x + 1]
+                )
+
+        def roots(lo, hi):
+            nc.scalar.activation(
+                out=rstd[:, 2 * lo : 2 * hi],
+                in_=ssq[:, 2 * lo : 2 * hi],
+                func=ACT.Abs_reciprocal_sqrt,
+                scale=1.0 / D,
+                bias=256.0 * 1e-5,
+            )
+
+        def finish(i):
+            c, q0, width, h = units[first + i]
+            for x in range(2):
+                nc.vector.scalar_tensor_tensor(
+                    out=o_sb[i][:, x, :],
+                    in0=y_cols(i, x),
+                    scalar=rstd[:, 2 * i + x : 2 * i + x + 1],
+                    in1=gn_sb[:],
+                    op0=MULT,
+                    op1=MULT,
+                )
+            nc.sync.dma_start(out=out[h, q0 : q0 + width, :].rearrange("(x p) e -> p x e", p=P), in_=o_sb[i][:])
+
+        round_q(0)
+        quantize_q(0)
+        round_k(0, 0, nc.vector.tensor_copy)
+        round_k(0, 1, nc.scalar.copy)
+        quantize_k(0, 0)
+        quantize_k(0, 1)
+        scale_mask(0, 0, 0, 128)
+        round_q(128)
+        quantize_q(128)
+
+        vector_extras = {
+            2: [lambda: round_q(256)],
+            3: [lambda: quantize_q(256), lambda: scale_mask(0, 128, 0, 128)],
+            5: [lambda: scale_mask(0, 256, 0, 256)],
+            6: [lambda: round_k(1, 0, nc.vector.tensor_copy)],
+            7: [lambda: round_k(1, 1, nc.vector.tensor_copy), lambda: quantize_k(1, 0)],
+            8: [lambda: quantize_k(1, 1)],
+            11: [lambda: scale_mask(1, 0, 0, 256)],
+            13: [lambda: quantize_v(0)],
+            14: [lambda: quantize_v(1), lambda: scale_mask(1, 0, 256, 512)],
+            15: [lambda: quantize_v(2)],
+            16: [lambda: quantize_v(3)],
+        }
+        scalar_extras = {9: 0, 11: 1, 12: 2, 14: 3}
+
+        done = 0
+        for u in range(len(units)):
+            last = max(k for k, fl in enumerate(fills) if fl[1] == u)
+            while done <= last:
+                fill(fills[done][1], fills[done][2])
+                done = done + 1
+            if u in scalar_extras:
+                round_v(scalar_extras[u])
+            for extra in vector_extras.get(u, []):
+                extra()
+            if u >= first + H:
+                second_product(u - first - H)
+                squares(u - first - H)
+            weigh(u)
+            if u > 0:
+                quantize_w(u - 1)
+        quantize_w(len(units) - 1)
+        roots(0, H)
+        for i in range(H, 2 * H):
+            second_product(i)
+        for i in range(H):
+            finish(i)
+        squares(H)
+        squares(H + 1)
+        roots(H, H + 2)
+        squares(H + 2)
+        squares(H + 3)
+        roots(H + 2, 2 * H)
+        for i in range(H, 2 * H):
+            finish(i)

@@ -21,7 +21,15 @@ BLK = 128
 BANK = 512
 SKEW = 3
 
-PHASES = [(0, 0, 128), (0, 128, 128), (0, 256, 256), (1, 0, 256), (1, 256, 256)]
+HALF = NQ // 2
+
+UNITS = (
+    [(0, 0, BLK, h) for h in range(H)]
+    + [(0, BLK, BLK, h) for h in range(H)]
+    + [(0, HALF, HALF, h) for h in range(H)]
+    + [(1, 0, HALF, h) for h in range(H)]
+    + [(1, HALF, HALF, h) for h in range(H)]
+)
 
 
 def tile_rows_a_tanh_kb_mask_onorm_kernel(tc, qT, kT, t, v, kb, mask, gn, out):
@@ -45,8 +53,6 @@ def tile_rows_a_tanh_kb_mask_onorm_kernel(tc, qT, kT, t, v, kb, mask, gn, out):
 
         kb_sb = sbuf("kb_sb", [P, 2, PACK], F32)
         t_sb = sbuf("t_sb", [P, 2, PACK], F32)
-        nc.scalar.dma_start(out=kb_sb[:], in_=kb.rearrange("(c p j) o -> p c (j o)", c=2, j=PACK))
-        nc.scalar.dma_start(out=t_sb[:], in_=t.rearrange("(c p j) o -> p c (j o)", c=2, j=PACK))
 
         q_raw, k_raw, v_raw, m_sb = {}, {}, {}, {}
 
@@ -67,28 +73,28 @@ def tile_rows_a_tanh_kb_mask_onorm_kernel(tc, qT, kT, t, v, kb, mask, gn, out):
             v_raw[h] = sbuf("v_raw%d" % h, [P, 2, PACK * D], F32)
             nc.sync.dma_start(out=v_raw[h][:], in_=v[h].rearrange("(c p j) e -> p c (j e)", c=2, j=PACK))
 
-        load_q(0, 128)
+        load_q(0, BLK)
         load_k(0)
-        load_mask(0, 0, 128)
-        load_q(128, 128)
-        load_mask(0, 128, 128)
-        load_q(256, 256)
-        load_mask(0, 256, 256)
+        nc.sync.dma_start(out=kb_sb[:], in_=kb.rearrange("(c p j) o -> p c (j o)", c=2, j=PACK))
+        nc.sync.dma_start(out=t_sb[:], in_=t.rearrange("(c p j) o -> p c (j o)", c=2, j=PACK))
+        load_mask(0, 0, BLK)
+        load_q(BLK, BLK)
+        load_mask(0, BLK, BLK)
+        load_q(HALF, HALF)
+        load_mask(0, HALF, HALF)
         load_k(1)
-        load_v(0)
-        load_v(1)
         load_mask(1, 0, NQ)
-        load_v(2)
-        load_v(3)
+        for h in range(H):
+            load_v(h)
         gn_sb = sbuf("gn_sb", [P, D], F32)
         nc.sync.dma_start(out=gn_sb[:], in_=gn[:, :])
 
         q_bf, q_mx, k_bf, k_mx, v_bf, v_mx = {}, {}, {}, {}, {}, {}
 
-        def round_q(q0):
+        def round_q(q0, copy):
             width = q_raw[q0].shape[2]
             q_bf[q0] = sbuf("q_bf%d" % q0, [P, width * PACK], BF16)
-            nc.vector.tensor_copy(
+            copy(
                 out=q_bf[q0][:].rearrange("p (g i j) -> p g j i", i=2, j=PACK),
                 in_=q_raw[q0][:].rearrange("p j (g i) -> p g j i", i=2),
             )
@@ -113,33 +119,31 @@ def tile_rows_a_tanh_kb_mask_onorm_kernel(tc, qT, kT, t, v, kb, mask, gn, out):
             for x in range(2):
                 k_mx[c, 2 * half + x] = (codes, scales, slice(x * P, (x + 1) * P))
 
-        def round_v(h):
-            v_bf[h] = sbuf("v_bf%d" % h, [P, 2 * D * PACK], BF16)
-            nc.scalar.copy(
-                out=v_bf[h][:].rearrange("p (c g i j) -> p c g j i", c=2, i=2, j=PACK),
-                in_=v_raw[h][:].rearrange("p c (j g i) -> p c g j i", j=PACK, i=2),
+        def round_v(h, c, copy):
+            if c == 0:
+                v_bf[h] = sbuf("v_bf%d" % h, [P, 2 * D * PACK], BF16)
+            copy(
+                out=v_bf[h][:, c * PASS : (c + 1) * PASS].rearrange("p (g i j) -> p g j i", i=2, j=PACK),
+                in_=v_raw[h][:, c, :].rearrange("p (j g i) -> p g j i", j=PACK, i=2),
             )
 
         def quantize_v(h):
             v_mx[h] = quantize("v%d" % h, v_bf[h][:], 2 * D)
 
-        def scale_mask(c, key, lo, hi):
-            for r in range(PACK):
-                rows = m_sb[c, key][:, r, lo:hi]
+        def scale_mask(c, key, slots):
+            for r in slots:
+                rows = m_sb[c, key][:, r, :]
                 nc.vector.tensor_scalar(out=rows, in0=rows, scalar1=t_sb[:, c, r : r + 1], scalar2=None, op0=MULT)
+
+        def scale_mask_scalar(c, key, slots):
+            for r in slots:
+                rows = m_sb[c, key][:, r, :]
+                nc.scalar.activation(out=rows, in_=rows, func=ACT.Copy, scale=t_sb[:, c, r : r + 1])
 
         score_bank = [psum.tile([P, BANK], F32, name="score%d" % h) for h in range(H)]
         y_bank = [psum.tile([P, BANK], F32, name="y%d" % b) for b in range(4)]
 
-        units = [(c, q0, width, h) for c, q0, width in PHASES for h in range(H)]
-        fills = []
-        base = 0
-        for u, (c, q0, width, h) in enumerate(units):
-            n = width // BLK
-            for f in range(n):
-                fills.append((base + SKEW * f, u, f))
-            base = base + n
-        fills = sorted(fills)
+        units = UNITS
         p_sb = [sbuf("p%d" % u, [P, PACK, unit[2]], F32) for u, unit in enumerate(units)]
 
         def fill(u, f):
@@ -169,27 +173,37 @@ def tile_rows_a_tanh_kb_mask_onorm_kernel(tc, qT, kT, t, v, kb, mask, gn, out):
                     bias=kb_sb[:, c, r : r + 1],
                 )
 
+        jobs = [(u, 0, unit[2]) for u, unit in enumerate(units)]
+        groups = [[0, 1, 2, 3], [4, 5, 6, 7], [8, 9], [10, 11], [12, 13], [14, 15], [16, 17], [18], [19]]
+        group_of = {j: g for g, members in enumerate(groups) for j in members}
         w_bf, w_mx = {}, {}
 
-        def weigh(u):
-            c, q0, width, h = units[u]
-            key = q0 if c == 0 else 0
-            mt = m_sb[c, key][:, :, q0 - key : q0 - key + width]
-            w_bf[u] = keep.tile([P, width * PACK], BF16, name="w_bf", tag="w_bf", bufs=4, align_bytes=64)
+        def weigh(j):
+            u, col, width = jobs[j]
+            c, q0, unit_width, h = units[u]
+            g = group_of[j]
+            if j == groups[g][0]:
+                w_bf[g] = keep.tile(
+                    [P, len(groups[g]) * width * PACK], BF16, name="w_bf", tag="w_bf", bufs=3, align_bytes=64
+                )
+            lo = (j - groups[g][0]) * width * PACK
             nc.vector.tensor_tensor(
-                out=w_bf[u][:].rearrange("p (g i r) -> p g r i", i=2, r=PACK),
-                in0=p_sb[u][:].rearrange("p r (g i) -> p g r i", i=2),
-                in1=mt.rearrange("p r (g i) -> p g r i", i=2),
+                out=w_bf[g][:, lo : lo + width * PACK].rearrange("p (g i r) -> p g r i", i=2, r=PACK),
+                in0=p_sb[u][:, :, col : col + width].rearrange("p r (g i) -> p g r i", i=2),
+                in1=m_sb[c, q0 * (1 - c)][:, :, q0 * c : q0 * c + width].rearrange("p r (g i) -> p g r i", i=2),
                 op=MULT,
             )
 
-        def quantize_w(u):
-            c, q0, width, h = units[u]
-            codes, scales = quantize("w%d" % u, w_bf[u][:], width)
-            for b in range(width // BLK):
-                w_mx[c, h, q0 // BLK + b] = (codes, scales, slice(b * BLK, (b + 1) * BLK))
+        def quantize_w(g):
+            width = jobs[groups[g][0]][2]
+            codes, scales = quantize("w%d" % g, w_bf[g][:], len(groups[g]) * width)
+            for n, j in enumerate(groups[g]):
+                u, col, width = jobs[j]
+                c, q0, unit_width, h = units[u]
+                for b in range(width // BLK):
+                    lo = n * width + b * BLK
+                    w_mx[c, h, (q0 + col) // BLK + b] = (codes, scales, slice(lo, lo + BLK))
 
-        first = 3 * H
         o_sb = [sbuf("o%d" % i, [P, 2, D], F32) for i in range(2 * H)]
         ssq = sbuf("ssq", [P, 4 * H], F32)
         rstd = sbuf("rstd", [P, 4 * H], F32)
@@ -199,7 +213,7 @@ def tile_rows_a_tanh_kb_mask_onorm_kernel(tc, qT, kT, t, v, kb, mask, gn, out):
             return y_bank[i // 2][:, lo : lo + D]
 
         def second_product(i):
-            c, q0, width, h = units[first + i]
+            h, q0 = i % H, (i // H) * HALF
             vc, vs = v_mx[h]
             for x in range(2):
                 for cc in range(2):
@@ -231,7 +245,7 @@ def tile_rows_a_tanh_kb_mask_onorm_kernel(tc, qT, kT, t, v, kb, mask, gn, out):
             )
 
         def finish(i):
-            c, q0, width, h = units[first + i]
+            h, q0 = i % H, (i // H) * HALF
             for x in range(2):
                 nc.vector.scalar_tensor_tensor(
                     out=o_sb[i][:, x, :],
@@ -241,60 +255,56 @@ def tile_rows_a_tanh_kb_mask_onorm_kernel(tc, qT, kT, t, v, kb, mask, gn, out):
                     op0=MULT,
                     op1=MULT,
                 )
-            nc.sync.dma_start(out=out[h, q0 : q0 + width, :].rearrange("(x p) e -> p x e", p=P), in_=o_sb[i][:])
+            nc.sync.dma_start(out=out[h, q0 : q0 + HALF, :].rearrange("(x p) e -> p x e", p=P), in_=o_sb[i][:])
 
-        round_q(0)
+        slots = range(PACK)
+        vcopy = nc.vector.tensor_copy
+        scopy = nc.scalar.copy
+
+        def scores(phase):
+            for f in range(units[phase * H][2] // BLK):
+                for h in range(H):
+                    fill(phase * H + h, f)
+
+        def weights(phase, side):
+            for h in range(H):
+                weigh(phase * H + h)
+                for job in side[h]:
+                    job()
+
+        round_q(0, vcopy)
         quantize_q(0)
-        round_k(0, 0, nc.vector.tensor_copy)
-        round_k(0, 1, nc.scalar.copy)
+        round_k(0, 0, vcopy)
+        round_k(0, 1, scopy)
         quantize_k(0, 0)
         quantize_k(0, 1)
-        scale_mask(0, 0, 0, 128)
-        round_q(128)
-        quantize_q(128)
-
-        vector_extras = {
-            2: [lambda: round_q(256)],
-            3: [lambda: quantize_q(256), lambda: scale_mask(0, 128, 0, 128)],
-            5: [lambda: scale_mask(0, 256, 0, 256)],
-            6: [lambda: round_k(1, 0, nc.vector.tensor_copy)],
-            7: [lambda: round_k(1, 1, nc.vector.tensor_copy), lambda: quantize_k(1, 0)],
-            8: [lambda: quantize_k(1, 1)],
-            11: [lambda: scale_mask(1, 0, 0, 256)],
-            13: [lambda: quantize_v(0)],
-            14: [lambda: quantize_v(1), lambda: scale_mask(1, 0, 256, 512)],
-            15: [lambda: quantize_v(2)],
-            16: [lambda: quantize_v(3)],
-        }
-        scalar_extras = {9: 0, 11: 1, 12: 2, 14: 3}
-
-        done = 0
-        for u in range(len(units)):
-            last = max(k for k, fl in enumerate(fills) if fl[1] == u)
-            while done <= last:
-                fill(fills[done][1], fills[done][2])
-                done = done + 1
-            if u in scalar_extras:
-                round_v(scalar_extras[u])
-            for extra in vector_extras.get(u, []):
-                extra()
-            if u >= first + H:
-                second_product(u - first - H)
-                squares(u - first - H)
-            weigh(u)
-            if u > 0:
-                quantize_w(u - 1)
-        quantize_w(len(units) - 1)
-        roots(0, H)
-        for i in range(H, 2 * H):
+        scale_mask(0, 0, slots)
+        round_q(BLK, vcopy)
+        scale_mask(0, BLK, slots)
+        quantize_q(BLK)
+        scores(0)
+        weights(0, [[], [lambda: round_q(HALF, vcopy)], [], [lambda: quantize_q(HALF)]])
+        scores(1)
+        weights(1, [[lambda: quantize_w(0), lambda: scale_mask(0, HALF, slots)], [lambda: round_k(1, 0, vcopy)], [lambda: round_k(1, 1, vcopy), lambda: quantize_k(1, 0)], [lambda: quantize_k(1, 1)]])
+        scores(2)
+        round_v(0, 0, scopy)
+        round_v(0, 1, scopy)
+        weights(2, [[lambda: quantize_w(1)], [lambda: quantize_v(0)], [lambda: scale_mask(1, 0, slots), lambda: quantize_w(2)], []])
+        scores(3)
+        round_v(1, 0, scopy)
+        round_v(1, 1, scopy)
+        round_v(2, 0, scopy)
+        round_v(2, 1, scopy)
+        weights(3, [[lambda: quantize_w(3)], [], [lambda: quantize_w(4), lambda: quantize_v(1)], [lambda: quantize_v(2)]])
+        scores(4)
+        round_v(3, 0, scopy)
+        round_v(3, 1, scopy)
+        weights(4, [[lambda: quantize_w(5)], [lambda: quantize_v(3)], [lambda: quantize_w(6)], [lambda: quantize_w(7), lambda: quantize_w(8)]])
+        for i in range(2 * H):
             second_product(i)
-        for i in range(H):
-            finish(i)
-        squares(H)
-        squares(H + 1)
-        roots(H, H + 2)
-        squares(H + 2)
-        squares(H + 3)
-        roots(H + 2, 2 * H)
-        for i in range(H, 2 * H):
+        for lo, hi in [(0, 2), (2, 4), (4, 6), (6, 8)]:
+            for i in range(lo, hi):
+                squares(i)
+            roots(lo, hi)
+        for i in range(2 * H):
             finish(i)

@@ -60,9 +60,9 @@ def tile_rows_a_tanh_kb_mask_onorm_kernel(tc, qT, kT, t, v, kb, mask, gn, out):
             q_raw[q0] = sbuf("q_raw%d" % q0, [P, PACK, width], F32)
             nc.sync.dma_start(out=q_raw[q0][:], in_=q_rows[:, :, q0 : q0 + width])
 
-        def load_k(c):
-            k_raw[c] = sbuf("k_raw%d" % c, [P, PACK, PASS], F32)
-            nc.sync.dma_start(out=k_raw[c][:], in_=k_rows[:, :, c * PASS : (c + 1) * PASS])
+        def load_k(c, lo, hi):
+            k_raw[c, lo] = sbuf("k_raw%d_%d" % (c, lo), [P, PACK, hi - lo], F32)
+            nc.sync.dma_start(out=k_raw[c, lo][:], in_=k_rows[:, :, c * PASS + lo : c * PASS + hi])
 
         def load_mask(c, q0, width):
             m_sb[c, q0] = sbuf("mask%d_%d" % (c, q0), [P, PACK, width], F32)
@@ -73,8 +73,9 @@ def tile_rows_a_tanh_kb_mask_onorm_kernel(tc, qT, kT, t, v, kb, mask, gn, out):
             v_raw[h] = sbuf("v_raw%d" % h, [P, 2, PACK * D], F32)
             nc.sync.dma_start(out=v_raw[h][:], in_=v[h].rearrange("(c p j) e -> p c (j e)", c=2, j=PACK))
 
+        load_k(0, 0, 384)
         load_q(0, BLK)
-        load_k(0)
+        load_k(0, 384, PASS)
         nc.sync.dma_start(out=kb_sb[:], in_=kb.rearrange("(c p j) o -> p c (j o)", c=2, j=PACK))
         nc.sync.dma_start(out=t_sb[:], in_=t.rearrange("(c p j) o -> p c (j o)", c=2, j=PACK))
         load_mask(0, 0, BLK)
@@ -82,7 +83,7 @@ def tile_rows_a_tanh_kb_mask_onorm_kernel(tc, qT, kT, t, v, kb, mask, gn, out):
         load_mask(0, BLK, BLK)
         load_q(HALF, HALF)
         load_mask(0, HALF, HALF)
-        load_k(1)
+        load_k(1, 0, PASS)
         load_mask(1, 0, NQ)
         for h in range(H):
             load_v(h)
@@ -106,11 +107,13 @@ def tile_rows_a_tanh_kb_mask_onorm_kernel(tc, qT, kT, t, v, kb, mask, gn, out):
                 cols = slice(b * BLK, (b + 1) * BLK)
                 q_mx[q0 // BLK + b] = (codes, scales, cols)
 
-        def round_k(c, half, copy):
-            k_bf[c, half] = sbuf("k_bf%d_%d" % (c, half), [P, 2 * P * PACK], BF16)
-            src = k_raw[c][:].rearrange("p j (s r) -> p s j r", r=PACK)
+        def round_k(c, half, copy, lo=0):
+            if lo == 0:
+                k_bf[c, half] = sbuf("k_bf%d_%d" % (c, half), [P, 2 * P * PACK], BF16)
+            src = k_raw[c, lo][:].rearrange("p j (s r) -> p s j r", r=PACK)
+            dst = k_bf[c, half][:].rearrange("p (r s j) -> p s j r", r=2, j=PACK)
             copy(
-                out=k_bf[c, half][:].rearrange("p (r s j) -> p s j r", r=2, j=PACK),
+                out=dst[:, lo // PACK : lo // PACK + src.shape[1]],
                 in_=src[:, :, :, 2 * half : 2 * half + 2],
             )
 
@@ -188,9 +191,9 @@ def tile_rows_a_tanh_kb_mask_onorm_kernel(tc, qT, kT, t, v, kb, mask, gn, out):
                 )
             lo = (j - groups[g][0]) * width * PACK
             nc.vector.tensor_tensor(
-                out=w_bf[g][:, lo : lo + width * PACK].rearrange("p (g i r) -> p g r i", i=2, r=PACK),
-                in0=p_sb[u][:, :, col : col + width].rearrange("p r (g i) -> p g r i", i=2),
-                in1=m_sb[c, q0 * (1 - c)][:, :, q0 * c : q0 * c + width].rearrange("p r (g i) -> p g r i", i=2),
+                out=w_bf[g][:, lo : lo + width * PACK].rearrange("p (g i r) -> p g r i", i=4, r=PACK),
+                in0=p_sb[u][:, :, col : col + width].rearrange("p r (g i) -> p g r i", i=4),
+                in1=m_sb[c, q0 * (1 - c)][:, :, q0 * c : q0 * c + width].rearrange("p r (g i) -> p g r i", i=4),
                 op=MULT,
             )
 
@@ -272,10 +275,12 @@ def tile_rows_a_tanh_kb_mask_onorm_kernel(tc, qT, kT, t, v, kb, mask, gn, out):
                 for job in side[h]:
                     job()
 
-        round_q(0, vcopy)
-        quantize_q(0)
         round_k(0, 0, vcopy)
         round_k(0, 1, scopy)
+        round_q(0, vcopy)
+        quantize_q(0)
+        round_k(0, 0, vcopy, 384)
+        round_k(0, 1, scopy, 384)
         quantize_k(0, 0)
         quantize_k(0, 1)
         scale_mask(0, 0, slots)

@@ -15,21 +15,25 @@ MULT = mybir.AluOpType.mult
 
 P = 128
 PACK = 4
-ROWS = 32
+ROWS = D // PACK
 PASS = P * PACK
+PASSES = N // PASS
 BLK = 128
 BANK = 512
-SKEW = 3
-
 HALF = NQ // 2
+PLACES = range(PACK)
 
-UNITS = (
-    [(0, 0, BLK, h) for h in range(H)]
-    + [(0, BLK, BLK, h) for h in range(H)]
-    + [(0, HALF, HALF, h) for h in range(H)]
-    + [(1, 0, HALF, h) for h in range(H)]
-    + [(1, HALF, HALF, h) for h in range(H)]
+K_FIRST = 384
+
+PHASES = [(0, 0, BLK), (0, BLK, BLK), (0, HALF, HALF), (1, 0, HALF), (1, HALF, HALF)]
+
+BATCHES = (
+    [(0, [0, 1, 2, 3]), (1, [0, 1, 2, 3])]
+    + [(phase, heads) for phase in [2, 3] for heads in [[0, 1], [2, 3]]]
+    + [(4, [0, 1]), (4, [2]), (4, [3])]
 )
+
+EPS = 256.0 * 1e-5
 
 
 def tile_rows_a_tanh_kb_mask_onorm_kernel(tc, qT, kT, t, v, kb, mask, gn, out):
@@ -50,11 +54,9 @@ def tile_rows_a_tanh_kb_mask_onorm_kernel(tc, qT, kT, t, v, kb, mask, gn, out):
 
         q_rows = qT.rearrange("h (p j) q -> (h p) j q", j=PACK)
         k_rows = kT.rearrange("h (p j) n -> (h p) j n", j=PACK)
-
-        kb_sb = sbuf("kb_sb", [P, 2, PACK], F32)
-        t_sb = sbuf("t_sb", [P, 2, PACK], F32)
-
-        q_raw, k_raw, v_raw, m_sb = {}, {}, {}, {}
+        kb_sb = sbuf("kb_sb", [P, PASSES, PACK], F32)
+        t_sb = sbuf("t_sb", [P, PASSES, PACK], F32)
+        q_raw, k_raw, v_raw, mask_sb = {}, {}, {}, {}
 
         def load_q(q0, width):
             q_raw[q0] = sbuf("q_raw%d" % q0, [P, PACK, width], F32)
@@ -65,19 +67,19 @@ def tile_rows_a_tanh_kb_mask_onorm_kernel(tc, qT, kT, t, v, kb, mask, gn, out):
             nc.sync.dma_start(out=k_raw[c, lo][:], in_=k_rows[:, :, c * PASS + lo : c * PASS + hi])
 
         def load_mask(c, q0, width):
-            m_sb[c, q0] = sbuf("mask%d_%d" % (c, q0), [P, PACK, width], F32)
-            rows = mask[c * PASS : (c + 1) * PASS, q0 : q0 + width]
-            nc.sync.dma_start(out=m_sb[c, q0][:], in_=rows.rearrange("(p j) q -> p j q", j=PACK))
+            mask_sb[c, q0] = sbuf("mask%d_%d" % (c, q0), [P, PACK, width], F32)
+            tokens = mask[c * PASS : (c + 1) * PASS, q0 : q0 + width]
+            nc.sync.dma_start(out=mask_sb[c, q0][:], in_=tokens.rearrange("(s r) q -> s r q", r=PACK))
 
         def load_v(h):
-            v_raw[h] = sbuf("v_raw%d" % h, [P, 2, PACK * D], F32)
-            nc.sync.dma_start(out=v_raw[h][:], in_=v[h].rearrange("(c p j) e -> p c (j e)", c=2, j=PACK))
+            v_raw[h] = sbuf("v_raw%d" % h, [P, PASSES, PACK * D], F32)
+            nc.sync.dma_start(out=v_raw[h][:], in_=v[h].rearrange("(c s r) e -> s c (r e)", c=PASSES, r=PACK))
 
-        load_k(0, 0, 384)
+        load_k(0, 0, K_FIRST)
         load_q(0, BLK)
-        load_k(0, 384, PASS)
-        nc.sync.dma_start(out=kb_sb[:], in_=kb.rearrange("(c p j) o -> p c (j o)", c=2, j=PACK))
-        nc.sync.dma_start(out=t_sb[:], in_=t.rearrange("(c p j) o -> p c (j o)", c=2, j=PACK))
+        load_k(0, K_FIRST, PASS)
+        nc.sync.dma_start(out=kb_sb[:], in_=kb.rearrange("(c s r) o -> s c (r o)", c=PASSES, r=PACK))
+        nc.sync.dma_start(out=t_sb[:], in_=t.rearrange("(c s r) o -> s c (r o)", c=PASSES, r=PACK))
         load_mask(0, 0, BLK)
         load_q(BLK, BLK)
         load_mask(0, BLK, BLK)
@@ -92,10 +94,10 @@ def tile_rows_a_tanh_kb_mask_onorm_kernel(tc, qT, kT, t, v, kb, mask, gn, out):
 
         q_bf, q_mx, k_bf, k_mx, v_bf, v_mx = {}, {}, {}, {}, {}, {}
 
-        def round_q(q0, copy):
+        def round_q(q0):
             width = q_raw[q0].shape[2]
             q_bf[q0] = sbuf("q_bf%d" % q0, [P, width * PACK], BF16)
-            copy(
+            nc.vector.tensor_copy(
                 out=q_bf[q0][:].rearrange("p (g i j) -> p g j i", i=2, j=PACK),
                 in_=q_raw[q0][:].rearrange("p j (g i) -> p g j i", i=2),
             )
@@ -104,212 +106,231 @@ def tile_rows_a_tanh_kb_mask_onorm_kernel(tc, qT, kT, t, v, kb, mask, gn, out):
             width = q_raw[q0].shape[2]
             codes, scales = quantize("q%d" % q0, q_bf[q0][:], width)
             for b in range(width // BLK):
-                cols = slice(b * BLK, (b + 1) * BLK)
-                q_mx[q0 // BLK + b] = (codes, scales, cols)
+                q_mx[q0 // BLK + b] = (codes, scales, slice(b * BLK, (b + 1) * BLK))
 
-        def round_k(c, half, copy, lo=0):
+        def round_k(c, pair, lo, copy):
             if lo == 0:
-                k_bf[c, half] = sbuf("k_bf%d_%d" % (c, half), [P, 2 * P * PACK], BF16)
+                k_bf[c, pair] = sbuf("k_bf%d_%d" % (c, pair), [P, 2 * P * PACK], BF16)
             src = k_raw[c, lo][:].rearrange("p j (s r) -> p s j r", r=PACK)
-            dst = k_bf[c, half][:].rearrange("p (r s j) -> p s j r", r=2, j=PACK)
+            dst = k_bf[c, pair][:].rearrange("p (r s j) -> p s j r", r=2, j=PACK)
             copy(
                 out=dst[:, lo // PACK : lo // PACK + src.shape[1]],
-                in_=src[:, :, :, 2 * half : 2 * half + 2],
+                in_=src[:, :, :, 2 * pair : 2 * pair + 2],
             )
 
-        def quantize_k(c, half):
-            codes, scales = quantize("k%d_%d" % (c, half), k_bf[c, half][:], 2 * P)
+        def quantize_k(c, pair):
+            codes, scales = quantize("k%d_%d" % (c, pair), k_bf[c, pair][:], 2 * P)
             for x in range(2):
-                k_mx[c, 2 * half + x] = (codes, scales, slice(x * P, (x + 1) * P))
+                k_mx[c, 2 * pair + x] = (codes, scales, slice(x * P, (x + 1) * P))
 
-        def round_v(h, c, copy):
-            if c == 0:
-                v_bf[h] = sbuf("v_bf%d" % h, [P, 2 * D * PACK], BF16)
-            copy(
-                out=v_bf[h][:, c * PASS : (c + 1) * PASS].rearrange("p (g i j) -> p g j i", i=2, j=PACK),
-                in_=v_raw[h][:, c, :].rearrange("p (j g i) -> p g j i", j=PACK, i=2),
+        def round_v(h):
+            v_bf[h] = sbuf("v_bf%d" % h, [P, PASSES * D * PACK], BF16)
+            nc.scalar.copy(
+                out=v_bf[h][:].rearrange("s (c g i r) -> s c g r i", c=PASSES, i=2, r=PACK),
+                in_=v_raw[h][:].rearrange("s c (r g i) -> s c g r i", r=PACK, i=2),
             )
 
         def quantize_v(h):
-            v_mx[h] = quantize("v%d" % h, v_bf[h][:], 2 * D)
+            codes, scales = quantize("v%d" % h, v_bf[h][:], PASSES * D)
+            for c in range(PASSES):
+                v_mx[h, c] = (codes, scales, slice(c * D, (c + 1) * D))
 
-        def scale_mask(c, key, slots):
-            for r in slots:
-                rows = m_sb[c, key][:, r, :]
-                nc.vector.tensor_scalar(out=rows, in0=rows, scalar1=t_sb[:, c, r : r + 1], scalar2=None, op0=MULT)
+        def scale_mask_on_vector(c, q0, places):
+            for r in places:
+                row = mask_sb[c, q0][:, r, :]
+                nc.vector.tensor_scalar(out=row, in0=row, scalar1=t_sb[:, c, r : r + 1], scalar2=None, op0=MULT)
 
-        def scale_mask_scalar(c, key, slots):
-            for r in slots:
-                rows = m_sb[c, key][:, r, :]
-                nc.scalar.activation(out=rows, in_=rows, func=ACT.Copy, scale=t_sb[:, c, r : r + 1])
+        def scale_mask_on_scalar(c, q0, places):
+            for r in places:
+                row = mask_sb[c, q0][:, r, :]
+                nc.scalar.activation(out=row, in_=row, func=ACT.Copy, scale=t_sb[:, c, r : r + 1])
+
+        def mx_product(dst, stationary, moving, rows, start, stop):
+            s_codes, s_scales, s_cols = stationary
+            m_codes, m_scales, m_cols = moving
+            nc.tensor.matmul_mx(
+                out=dst,
+                lhsT=s_codes[rows, s_cols].bitcast(FP8X4),
+                lhsT_scale=s_scales[rows, s_cols],
+                rhs=m_codes[rows, m_cols].bitcast(FP8X4),
+                rhs_scale=m_scales[rows, m_cols],
+                start=start,
+                stop=stop,
+            )
 
         score_bank = [psum.tile([P, BANK], F32, name="score%d" % h) for h in range(H)]
-        y_bank = [psum.tile([P, BANK], F32, name="y%d" % b) for b in range(4)]
+        y_bank = [psum.tile([P, BANK], F32, name="y%d" % b) for b in range(H * (NQ // BLK) * D // BANK)]
+        p_sb = {}
+        for phase, (c, q0, width) in enumerate(PHASES):
+            for h in range(H):
+                p_sb[phase, h] = sbuf("p%d_%d" % (phase, h), [P, PACK, width], F32)
 
-        units = UNITS
-        p_sb = [sbuf("p%d" % u, [P, PACK, unit[2]], F32) for u, unit in enumerate(units)]
+        def scores(phase):
+            c, q0, width = PHASES[phase]
+            per_bank = BANK // width
+            for first in range(0, PACK, per_bank):
+                for h in range(H):
+                    rows = slice(ROWS * h, ROWS * (h + 1))
+                    for x in range(per_bank):
+                        for b in range(width // BLK):
+                            lo = x * width + b * BLK
+                            dst = score_bank[h][:, lo : lo + BLK]
+                            mx_product(dst, k_mx[c, first + x], q_mx[q0 // BLK + b], rows, True, True)
+                    for x in range(per_bank):
+                        r = first + x
+                        nc.scalar.activation(
+                            out=p_sb[phase, h][:, r, :],
+                            in_=score_bank[h][:, x * width : (x + 1) * width],
+                            func=ACT.Tanh,
+                            bias=kb_sb[:, c, r : r + 1],
+                        )
 
-        def fill(u, f):
-            c, q0, width, h = units[u]
-            rows = slice(ROWS * h, ROWS * (h + 1))
-            slots = BANK // width
-            for x in range(slots):
-                kc, ks, kcols = k_mx[c, f * slots + x]
-                for b in range(width // BLK):
-                    qc, qs, qcols = q_mx[q0 // BLK + b]
-                    lo = x * width + b * BLK
-                    nc.tensor.matmul_mx(
-                        out=score_bank[h][:, lo : lo + BLK],
-                        lhsT=kc[rows, kcols].bitcast(FP8X4),
-                        lhsT_scale=ks[rows, kcols],
-                        rhs=qc[rows, qcols].bitcast(FP8X4),
-                        rhs_scale=qs[rows, qcols],
-                        start=True,
-                        stop=True,
-                    )
-            for x in range(slots):
-                r = f * slots + x
-                nc.scalar.activation(
-                    out=p_sb[u][:, r, :],
-                    in_=score_bank[h][:, x * width : (x + 1) * width],
-                    func=ACT.Tanh,
-                    bias=kb_sb[:, c, r : r + 1],
-                )
-
-        jobs = [(u, 0, unit[2]) for u, unit in enumerate(units)]
-        groups = [[0, 1, 2, 3], [4, 5, 6, 7], [8, 9], [10, 11], [12, 13], [14, 15], [16, 17], [18], [19]]
-        group_of = {j: g for g, members in enumerate(groups) for j in members}
+        batch_of = {(phase, h): n for n, (phase, heads) in enumerate(BATCHES) for h in heads}
         w_bf, w_mx = {}, {}
 
-        def weigh(j):
-            u, col, width = jobs[j]
-            c, q0, unit_width, h = units[u]
-            g = group_of[j]
-            if j == groups[g][0]:
-                w_bf[g] = keep.tile(
-                    [P, len(groups[g]) * width * PACK], BF16, name="w_bf", tag="w_bf", bufs=3, align_bytes=64
+        def weigh(phase, h):
+            c, q0, width = PHASES[phase]
+            n = batch_of[phase, h]
+            heads = BATCHES[n][1]
+            if h == heads[0]:
+                w_bf[n] = keep.tile(
+                    [P, len(heads) * width * PACK], BF16, name="w_bf", tag="w_bf", bufs=3, align_bytes=64
                 )
-            lo = (j - groups[g][0]) * width * PACK
+            lo = (h - heads[0]) * width * PACK
+            scaled = mask_sb[0, q0][:] if c == 0 else mask_sb[1, 0][:, :, q0 : q0 + width]
             nc.vector.tensor_tensor(
-                out=w_bf[g][:, lo : lo + width * PACK].rearrange("p (g i r) -> p g r i", i=4, r=PACK),
-                in0=p_sb[u][:, :, col : col + width].rearrange("p r (g i) -> p g r i", i=4),
-                in1=m_sb[c, q0 * (1 - c)][:, :, q0 * c : q0 * c + width].rearrange("p r (g i) -> p g r i", i=4),
+                out=w_bf[n][:, lo : lo + width * PACK].rearrange("s (g i r) -> s g r i", i=4, r=PACK),
+                in0=p_sb[phase, h][:].rearrange("s r (g i) -> s g r i", i=4),
+                in1=scaled.rearrange("s r (g i) -> s g r i", i=4),
                 op=MULT,
             )
 
-        def quantize_w(g):
-            width = jobs[groups[g][0]][2]
-            codes, scales = quantize("w%d" % g, w_bf[g][:], len(groups[g]) * width)
-            for n, j in enumerate(groups[g]):
-                u, col, width = jobs[j]
-                c, q0, unit_width, h = units[u]
+        def quantize_w(n):
+            phase, heads = BATCHES[n]
+            c, q0, width = PHASES[phase]
+            codes, scales = quantize("w%d" % n, w_bf[n][:], len(heads) * width)
+            for h in heads:
                 for b in range(width // BLK):
-                    lo = n * width + b * BLK
-                    w_mx[c, h, (q0 + col) // BLK + b] = (codes, scales, slice(lo, lo + BLK))
+                    lo = (h - heads[0]) * width + b * BLK
+                    w_mx[c, h, q0 // BLK + b] = (codes, scales, slice(lo, lo + BLK))
 
-        o_sb = [sbuf("o%d" % i, [P, 2, D], F32) for i in range(2 * H)]
-        ssq = sbuf("ssq", [P, 4 * H], F32)
-        rstd = sbuf("rstd", [P, 4 * H], F32)
+        pieces = 2 * H
+        o_sb = [sbuf("o%d" % i, [P, 2, D], F32) for i in range(pieces)]
+        ssq = sbuf("ssq", [P, 2 * pieces], F32)
+        rstd = sbuf("rstd", [P, 2 * pieces], F32)
 
         def y_cols(i, x):
-            lo = (i % 2) * 2 * D + x * D
+            lo = ((i % 2) * 2 + x) * D
             return y_bank[i // 2][:, lo : lo + D]
 
         def second_product(i):
-            h, q0 = i % H, (i // H) * HALF
-            vc, vs = v_mx[h]
+            h, half = i % H, i // H
             for x in range(2):
-                for cc in range(2):
-                    wc, ws, wcols = w_mx[cc, h, q0 // BLK + x]
-                    vcols = slice(cc * D, (cc + 1) * D)
-                    nc.tensor.matmul_mx(
-                        out=y_cols(i, x),
-                        lhsT=wc[:, wcols].bitcast(FP8X4),
-                        lhsT_scale=ws[:, wcols],
-                        rhs=vc[:, vcols].bitcast(FP8X4),
-                        rhs_scale=vs[:, vcols],
-                        start=(cc == 0),
-                        stop=(cc == 1),
-                    )
+                for c in range(PASSES):
+                    weights = w_mx[c, h, 2 * half + x]
+                    mx_product(y_cols(i, x), weights, v_mx[h, c], slice(0, P), c == 0, c == PASSES - 1)
 
         def squares(i):
             for x in range(2):
+                col = 2 * i + x
                 nc.scalar.activation(
-                    out=o_sb[i][:, x, :], in_=y_cols(i, x), func=ACT.Square, accum_out=ssq[:, 2 * i + x : 2 * i + x + 1]
+                    out=o_sb[i][:, x, :], in_=y_cols(i, x), func=ACT.Square, accum_out=ssq[:, col : col + 1]
                 )
 
-        def roots(lo, hi):
+        def roots(bank):
+            cols = slice(4 * bank, 4 * (bank + 1))
             nc.scalar.activation(
-                out=rstd[:, 2 * lo : 2 * hi],
-                in_=ssq[:, 2 * lo : 2 * hi],
-                func=ACT.Abs_reciprocal_sqrt,
-                scale=1.0 / D,
-                bias=256.0 * 1e-5,
+                out=rstd[:, cols], in_=ssq[:, cols], func=ACT.Abs_reciprocal_sqrt, scale=1.0 / D, bias=EPS
             )
 
         def finish(i):
             h, q0 = i % H, (i // H) * HALF
             for x in range(2):
+                col = 2 * i + x
                 nc.vector.scalar_tensor_tensor(
                     out=o_sb[i][:, x, :],
                     in0=y_cols(i, x),
-                    scalar=rstd[:, 2 * i + x : 2 * i + x + 1],
+                    scalar=rstd[:, col : col + 1],
                     in1=gn_sb[:],
                     op0=MULT,
                     op1=MULT,
                 )
             nc.sync.dma_start(out=out[h, q0 : q0 + HALF, :].rearrange("(x p) e -> p x e", p=P), in_=o_sb[i][:])
 
-        slots = range(PACK)
-        vcopy = nc.vector.tensor_copy
-        scopy = nc.scalar.copy
-
-        def scores(phase):
-            for f in range(units[phase * H][2] // BLK):
-                for h in range(H):
-                    fill(phase * H + h, f)
-
-        def weights(phase, side):
-            for h in range(H):
-                weigh(phase * H + h)
-                for job in side[h]:
-                    job()
-
-        round_k(0, 0, vcopy)
-        round_k(0, 1, scopy)
-        round_q(0, vcopy)
+        round_k(0, 0, 0, nc.vector.tensor_copy)
+        round_k(0, 1, 0, nc.scalar.copy)
+        round_q(0)
         quantize_q(0)
-        round_k(0, 0, vcopy, 384)
-        round_k(0, 1, scopy, 384)
+        round_k(0, 0, K_FIRST, nc.vector.tensor_copy)
+        round_k(0, 1, K_FIRST, nc.scalar.copy)
         quantize_k(0, 0)
         quantize_k(0, 1)
-        scale_mask(0, 0, slots)
-        round_q(BLK, vcopy)
-        scale_mask(0, BLK, slots)
+        scale_mask_on_scalar(0, 0, PLACES)
+        round_q(BLK)
+        scale_mask_on_vector(0, BLK, PLACES)
         quantize_q(BLK)
+
         scores(0)
-        weights(0, [[], [lambda: round_q(HALF, vcopy)], [], [lambda: quantize_q(HALF)]])
+        weigh(0, 0)
+        weigh(0, 1)
+        round_q(HALF)
+        weigh(0, 2)
+        weigh(0, 3)
+        quantize_q(HALF)
+
         scores(1)
-        weights(1, [[lambda: quantize_w(0), lambda: scale_mask(0, HALF, slots)], [lambda: round_k(1, 0, vcopy)], [lambda: round_k(1, 1, vcopy), lambda: quantize_k(1, 0)], [lambda: quantize_k(1, 1)]])
+        weigh(1, 0)
+        quantize_w(0)
+        scale_mask_on_vector(0, HALF, PLACES)
+        weigh(1, 1)
+        round_k(1, 0, 0, nc.vector.tensor_copy)
+        weigh(1, 2)
+        round_k(1, 1, 0, nc.vector.tensor_copy)
+        quantize_k(1, 0)
+        weigh(1, 3)
+        quantize_k(1, 1)
+
         scores(2)
-        round_v(0, 0, scopy)
-        round_v(0, 1, scopy)
-        weights(2, [[lambda: quantize_w(1)], [lambda: quantize_v(0)], [lambda: scale_mask(1, 0, slots), lambda: quantize_w(2)], []])
+        scale_mask_on_scalar(1, 0, PLACES[:1])
+        round_v(0)
+        weigh(2, 0)
+        quantize_w(1)
+        weigh(2, 1)
+        quantize_v(0)
+        weigh(2, 2)
+        scale_mask_on_vector(1, 0, PLACES[1:])
+        quantize_w(2)
+        weigh(2, 3)
+
         scores(3)
-        round_v(1, 0, scopy)
-        round_v(1, 1, scopy)
-        round_v(2, 0, scopy)
-        round_v(2, 1, scopy)
-        weights(3, [[lambda: quantize_w(3)], [], [lambda: quantize_w(4), lambda: quantize_v(1)], [lambda: quantize_v(2)]])
+        round_v(1)
+        round_v(2)
+        weigh(3, 0)
+        quantize_w(3)
+        weigh(3, 1)
+        weigh(3, 2)
+        quantize_w(4)
+        quantize_v(1)
+        weigh(3, 3)
+        quantize_v(2)
+
         scores(4)
-        round_v(3, 0, scopy)
-        round_v(3, 1, scopy)
-        weights(4, [[lambda: quantize_w(5)], [lambda: quantize_v(3)], [lambda: quantize_w(6)], [lambda: quantize_w(7), lambda: quantize_w(8)]])
-        for i in range(2 * H):
+        round_v(3)
+        weigh(4, 0)
+        quantize_w(5)
+        weigh(4, 1)
+        quantize_v(3)
+        weigh(4, 2)
+        quantize_w(6)
+        weigh(4, 3)
+        quantize_w(7)
+        quantize_w(8)
+
+        for i in range(pieces):
             second_product(i)
-        for lo, hi in [(0, 2), (2, 4), (4, 6), (6, 8)]:
-            for i in range(lo, hi):
-                squares(i)
-            roots(lo, hi)
-        for i in range(2 * H):
+        for bank in range(len(y_bank)):
+            squares(2 * bank)
+            squares(2 * bank + 1)
+            roots(bank)
+        for i in range(pieces):
             finish(i)

from contextlib import ExitStack

import concourse.mybir as mybir

H, D, NQ, N = 4, 128, 512, 1024
FLOPS = 2 * 2 * H * N * NQ * D

F32 = mybir.dt.float32
BF16 = mybir.dt.bfloat16
U32 = mybir.dt.uint32
U8 = mybir.dt.uint8
FP8X4 = mybir.dt.float8_e4m3fn_x4
ACT = mybir.ActivationFunctionType
MULT = mybir.AluOpType.mult

P = 128
PACK = 4
ROWS = D // PACK
PASS = P * PACK
PASSES = N // PASS
BLK = 128
BANK = 512
HALF = NQ // 2
PLACES = range(PACK)

K_FIRST = 384

PHASES = [(0, 0, BLK), (0, BLK, BLK), (0, HALF, HALF), (1, 0, HALF), (1, HALF, HALF)]

BATCHES = (
    [(0, [0, 1, 2, 3]), (1, [0, 1, 2, 3])]
    + [(phase, heads) for phase in [2, 3] for heads in [[0, 1], [2, 3]]]
    + [(4, [0, 1]), (4, [2]), (4, [3])]
)

EPS = 256.0 * 1e-5


def tile_rows_a_tanh_kb_mask_onorm_kernel(tc, qT, kT, t, v, kb, mask, gn, out):
    nc = tc.nc
    with ExitStack() as ctx:
        keep = ctx.enter_context(tc.tile_pool(name="keep", bufs=1))
        psum = ctx.enter_context(tc.psum_pool(name="psum", bufs=1))
        ctx.enter_context(tc.manual_schedule())

        def sbuf(name, shape, dtype):
            return keep.tile(shape, dtype, name=name, align_bytes=64)

        def quantize(name, staged, words):
            codes = sbuf(name + "_codes", [P, words], U32)
            scales = sbuf(name + "_scales", [P, words], U8)
            nc.vector.quantize_mx(out=codes[:].bitcast(FP8X4), scales=scales[:], in_=staged)
            return codes, scales

        q_rows = qT.rearrange("h (p j) q -> (h p) j q", j=PACK)
        k_rows = kT.rearrange("h (p j) n -> (h p) j n", j=PACK)
        kb_sb = sbuf("kb_sb", [P, PASSES, PACK], F32)
        t_sb = sbuf("t_sb", [P, PASSES, PACK], F32)
        q_raw, k_raw, v_raw, mask_sb = {}, {}, {}, {}

        def load_q(q0, width):
            q_raw[q0] = sbuf("q_raw%d" % q0, [P, PACK, width], F32)
            nc.sync.dma_start(out=q_raw[q0][:], in_=q_rows[:, :, q0 : q0 + width])

        def load_k(c, lo, hi):
            k_raw[c, lo] = sbuf("k_raw%d_%d" % (c, lo), [P, PACK, hi - lo], F32)
            nc.sync.dma_start(out=k_raw[c, lo][:], in_=k_rows[:, :, c * PASS + lo : c * PASS + hi])

        def load_mask(c, q0, width):
            mask_sb[c, q0] = sbuf("mask%d_%d" % (c, q0), [P, PACK, width], F32)
            tokens = mask[c * PASS : (c + 1) * PASS, q0 : q0 + width]
            nc.sync.dma_start(out=mask_sb[c, q0][:], in_=tokens.rearrange("(s r) q -> s r q", r=PACK))

        def load_v(h):
            v_raw[h] = sbuf("v_raw%d" % h, [P, PASSES, PACK * D], F32)
            nc.sync.dma_start(out=v_raw[h][:], in_=v[h].rearrange("(c s r) e -> s c (r e)", c=PASSES, r=PACK))

        load_k(0, 0, K_FIRST)
        load_q(0, BLK)
        load_k(0, K_FIRST, PASS)
        nc.sync.dma_start(out=kb_sb[:], in_=kb.rearrange("(c s r) o -> s c (r o)", c=PASSES, r=PACK))
        nc.sync.dma_start(out=t_sb[:], in_=t.rearrange("(c s r) o -> s c (r o)", c=PASSES, r=PACK))
        load_mask(0, 0, BLK)
        load_q(BLK, BLK)
        load_mask(0, BLK, BLK)
        load_q(HALF, HALF)
        load_mask(0, HALF, HALF)
        load_k(1, 0, PASS)
        load_mask(1, 0, NQ)
        for h in range(H):
            load_v(h)
        gn_sb = sbuf("gn_sb", [P, D], F32)
        nc.sync.dma_start(out=gn_sb[:], in_=gn[:, :])

        q_bf, q_mx, k_bf, k_mx, v_bf, v_mx = {}, {}, {}, {}, {}, {}

        def round_q(q0):
            width = q_raw[q0].shape[2]
            q_bf[q0] = sbuf("q_bf%d" % q0, [P, width * PACK], BF16)
            nc.vector.tensor_copy(
                out=q_bf[q0][:].rearrange("p (g i j) -> p g j i", i=2, j=PACK),
                in_=q_raw[q0][:].rearrange("p j (g i) -> p g j i", i=2),
            )

        def quantize_q(q0):
            width = q_raw[q0].shape[2]
            codes, scales = quantize("q%d" % q0, q_bf[q0][:], width)
            for b in range(width // BLK):
                q_mx[q0 // BLK + b] = (codes, scales, slice(b * BLK, (b + 1) * BLK))

        def round_k(c, pair, lo, copy):
            if lo == 0:
                k_bf[c, pair] = sbuf("k_bf%d_%d" % (c, pair), [P, 2 * P * PACK], BF16)
            src = k_raw[c, lo][:].rearrange("p j (s r) -> p s j r", r=PACK)
            dst = k_bf[c, pair][:].rearrange("p (r s j) -> p s j r", r=2, j=PACK)
            copy(
                out=dst[:, lo // PACK : lo // PACK + src.shape[1]],
                in_=src[:, :, :, 2 * pair : 2 * pair + 2],
            )

        def quantize_k(c, pair):
            codes, scales = quantize("k%d_%d" % (c, pair), k_bf[c, pair][:], 2 * P)
            for x in range(2):
                k_mx[c, 2 * pair + x] = (codes, scales, slice(x * P, (x + 1) * P))

        def round_v(h):
            v_bf[h] = sbuf("v_bf%d" % h, [P, PASSES * D * PACK], BF16)
            nc.scalar.copy(
                out=v_bf[h][:].rearrange("s (c g i r) -> s c g r i", c=PASSES, i=2, r=PACK),
                in_=v_raw[h][:].rearrange("s c (r g i) -> s c g r i", r=PACK, i=2),
            )

        def quantize_v(h):
            codes, scales = quantize("v%d" % h, v_bf[h][:], PASSES * D)
            for c in range(PASSES):
                v_mx[h, c] = (codes, scales, slice(c * D, (c + 1) * D))

        def scale_mask_on_vector(c, q0, places):
            for r in places:
                row = mask_sb[c, q0][:, r, :]
                nc.vector.tensor_scalar(out=row, in0=row, scalar1=t_sb[:, c, r : r + 1], scalar2=None, op0=MULT)

        def scale_mask_on_scalar(c, q0, places):
            for r in places:
                row = mask_sb[c, q0][:, r, :]
                nc.scalar.activation(out=row, in_=row, func=ACT.Copy, scale=t_sb[:, c, r : r + 1])

        def mx_product(dst, stationary, moving, rows, start, stop):
            s_codes, s_scales, s_cols = stationary
            m_codes, m_scales, m_cols = moving
            nc.tensor.matmul_mx(
                out=dst,
                lhsT=s_codes[rows, s_cols].bitcast(FP8X4),
                lhsT_scale=s_scales[rows, s_cols],
                rhs=m_codes[rows, m_cols].bitcast(FP8X4),
                rhs_scale=m_scales[rows, m_cols],
                start=start,
                stop=stop,
            )

        score_bank = [psum.tile([P, BANK], F32, name="score%d" % h) for h in range(H)]
        y_bank = [psum.tile([P, BANK], F32, name="y%d" % b) for b in range(H * (NQ // BLK) * D // BANK)]
        p_sb = {}
        for phase, (c, q0, width) in enumerate(PHASES):
            for h in range(H):
                p_sb[phase, h] = sbuf("p%d_%d" % (phase, h), [P, PACK, width], F32)

        def scores(phase):
            c, q0, width = PHASES[phase]
            per_bank = BANK // width
            for first in range(0, PACK, per_bank):
                for h in range(H):
                    rows = slice(ROWS * h, ROWS * (h + 1))
                    for x in range(per_bank):
                        for b in range(width // BLK):
                            lo = x * width + b * BLK
                            dst = score_bank[h][:, lo : lo + BLK]
                            mx_product(dst, k_mx[c, first + x], q_mx[q0 // BLK + b], rows, True, True)
                    for x in range(per_bank):
                        r = first + x
                        nc.scalar.activation(
                            out=p_sb[phase, h][:, r, :],
                            in_=score_bank[h][:, x * width : (x + 1) * width],
                            func=ACT.Tanh,
                            bias=kb_sb[:, c, r : r + 1],
                        )

        batch_of = {(phase, h): n for n, (phase, heads) in enumerate(BATCHES) for h in heads}
        w_bf, w_mx = {}, {}

        def weigh(phase, h):
            c, q0, width = PHASES[phase]
            n = batch_of[phase, h]
            heads = BATCHES[n][1]
            if h == heads[0]:
                w_bf[n] = keep.tile(
                    [P, len(heads) * width * PACK], BF16, name="w_bf", tag="w_bf", bufs=3, align_bytes=64
                )
            lo = (h - heads[0]) * width * PACK
            scaled = mask_sb[0, q0][:] if c == 0 else mask_sb[1, 0][:, :, q0 : q0 + width]
            nc.vector.tensor_tensor(
                out=w_bf[n][:, lo : lo + width * PACK].rearrange("s (g i r) -> s g r i", i=4, r=PACK),
                in0=p_sb[phase, h][:].rearrange("s r (g i) -> s g r i", i=4),
                in1=scaled.rearrange("s r (g i) -> s g r i", i=4),
                op=MULT,
            )

        def quantize_w(n):
            phase, heads = BATCHES[n]
            c, q0, width = PHASES[phase]
            codes, scales = quantize("w%d" % n, w_bf[n][:], len(heads) * width)
            for h in heads:
                for b in range(width // BLK):
                    lo = (h - heads[0]) * width + b * BLK
                    w_mx[c, h, q0 // BLK + b] = (codes, scales, slice(lo, lo + BLK))

        pieces = 2 * H
        o_sb = [sbuf("o%d" % i, [P, 2, D], F32) for i in range(pieces)]
        ssq = sbuf("ssq", [P, 2 * pieces], F32)
        rstd = sbuf("rstd", [P, 2 * pieces], F32)

        def y_cols(i, x):
            lo = ((i % 2) * 2 + x) * D
            return y_bank[i // 2][:, lo : lo + D]

        def second_product(i):
            h, half = i % H, i // H
            for x in range(2):
                for c in range(PASSES):
                    weights = w_mx[c, h, 2 * half + x]
                    mx_product(y_cols(i, x), weights, v_mx[h, c], slice(0, P), c == 0, c == PASSES - 1)

        def squares(i):
            for x in range(2):
                col = 2 * i + x
                nc.scalar.activation(
                    out=o_sb[i][:, x, :], in_=y_cols(i, x), func=ACT.Square, accum_out=ssq[:, col : col + 1]
                )

        def roots(bank):
            cols = slice(4 * bank, 4 * (bank + 1))
            nc.scalar.activation(
                out=rstd[:, cols], in_=ssq[:, cols], func=ACT.Abs_reciprocal_sqrt, scale=1.0 / D, bias=EPS
            )

        def finish(i):
            h, q0 = i % H, (i // H) * HALF
            for x in range(2):
                col = 2 * i + x
                nc.vector.scalar_tensor_tensor(
                    out=o_sb[i][:, x, :],
                    in0=y_cols(i, x),
                    scalar=rstd[:, col : col + 1],
                    in1=gn_sb[:],
                    op0=MULT,
                    op1=MULT,
                )
            nc.sync.dma_start(out=out[h, q0 : q0 + HALF, :].rearrange("(x p) e -> p x e", p=P), in_=o_sb[i][:])

        round_k(0, 0, 0, nc.vector.tensor_copy)
        round_k(0, 1, 0, nc.scalar.copy)
        round_q(0)
        quantize_q(0)
        round_k(0, 0, K_FIRST, nc.vector.tensor_copy)
        round_k(0, 1, K_FIRST, nc.scalar.copy)
        quantize_k(0, 0)
        quantize_k(0, 1)
        scale_mask_on_scalar(0, 0, PLACES)
        round_q(BLK)
        scale_mask_on_vector(0, BLK, PLACES)
        quantize_q(BLK)

        scores(0)
        weigh(0, 0)
        weigh(0, 1)
        round_q(HALF)
        weigh(0, 2)
        weigh(0, 3)
        quantize_q(HALF)

        scores(1)
        weigh(1, 0)
        quantize_w(0)
        scale_mask_on_vector(0, HALF, PLACES)
        weigh(1, 1)
        round_k(1, 0, 0, nc.vector.tensor_copy)
        weigh(1, 2)
        round_k(1, 1, 0, nc.vector.tensor_copy)
        quantize_k(1, 0)
        weigh(1, 3)
        quantize_k(1, 1)

        scores(2)
        scale_mask_on_scalar(1, 0, PLACES[:1])
        round_v(0)
        weigh(2, 0)
        quantize_w(1)
        weigh(2, 1)
        quantize_v(0)
        weigh(2, 2)
        scale_mask_on_vector(1, 0, PLACES[1:])
        quantize_w(2)
        weigh(2, 3)

        scores(3)
        round_v(1)
        round_v(2)
        weigh(3, 0)
        quantize_w(3)
        weigh(3, 1)
        weigh(3, 2)
        quantize_w(4)
        quantize_v(1)
        weigh(3, 3)
        quantize_v(2)

        scores(4)
        round_v(3)
        weigh(4, 0)
        quantize_w(5)
        weigh(4, 1)
        quantize_v(3)
        weigh(4, 2)
        quantize_w(6)
        weigh(4, 3)
        quantize_w(7)
        quantize_w(8)

        for i in range(pieces):
            second_product(i)
        for bank in range(len(y_bank)):
            squares(2 * bank)
            squares(2 * bank + 1)
            roots(bank)
        for i in range(pieces):
            finish(i)
